import numpy as np
import ml_dtypes


def mxq(x, axis, fmt="e4m3"):
    dtype, down = {"e4m3": (ml_dtypes.float8_e4m3fn, 7), "e5m2": (ml_dtypes.float8_e5m2, 14)}[fmt]
    v = np.moveaxis(np.asarray(x, np.float32).astype(ml_dtypes.bfloat16).astype(np.float64), axis, -1)
    blocks = v.reshape(v.shape[:-1] + (-1, 32))
    amax = np.abs(blocks).max(-1, keepdims=True)
    byte = np.maximum(np.where(amax > 0, np.frexp(amax)[1] - 1 + 127, 0) - down, 1)
    scale = np.exp2(byte - 127.0)
    codes = (blocks / scale).astype(np.float32).astype(dtype).astype(np.float64)
    return np.moveaxis((codes * scale).reshape(v.shape), -1, axis)


WIDE = False


def mx_kscale(k):
    if not WIDE:
        return np.ones(k)
    levels = np.array([10, -10, 5, -5, 0])
    if k % 512:
        return np.exp2(np.random.permutation(np.resize(levels, k // 32))).repeat(32)
    a = np.empty((k // 512, 16))
    for p in range(k // 512):
        a[p, :8] = np.random.permutation(np.resize(levels, 8))
        for g in range(8):
            far = levels[np.abs(levels - a[p, g]) >= 10]
            a[p, g + 8] = far[np.random.randint(len(far))]
    return np.exp2(a.ravel()).repeat(32)


def f64(x):
    return np.asarray(x).astype(np.float64)


def striped(idx):
    return np.tile(idx.reshape(-1, 16).T, (8, 1)).astype(np.uint16)


def unstriped(offs):
    return offs[:16].T.reshape(-1).astype(np.int64)


def pack_weight(w):
    k, n = w.shape
    w = f64(np.asarray(w, np.float32).astype(ml_dtypes.bfloat16)).reshape(k // 32, 32, n)
    amax = np.abs(w).max(1)
    byte = np.clip(np.where(amax > 0, np.frexp(amax)[1] - 1 + 127 - 7, 1), 1, 254)
    scaled = (w * np.exp2(127.0 - byte)[:, None, :]).reshape(k, n).astype(np.float32)
    words = np.ascontiguousarray(scaled.reshape(k // 512, 128, 4, n).transpose(0, 1, 3, 2)).astype(ml_dtypes.float8_e4m3fn).view(np.uint8)
    return words, np.ascontiguousarray(byte.astype(np.uint8).reshape(k // 512, 16, n))


def unpack_weight(words, scales):
    g, p, n, _ = words.shape
    vals = np.ascontiguousarray(words).view(ml_dtypes.float8_e4m3fn).astype(np.float64) * np.repeat(np.exp2(scales.astype(np.float64) - 127.0), 8, axis=1)[..., None]
    return vals.transpose(0, 1, 3, 2).reshape(g * 512, n)


K, T, S, N, D, U, V, W = 512, 1024, 512, 256, 4, 1024, 256, 256


def setup_inputs():
    n = np.random.standard_normal
    s = mx_kscale(K)[:, None]
    packed_xT = pack_weight(n((K, T)) * s)
    return {
        "x_words": packed_xT[0],
        "x_scales": packed_xT[1],
        "w1": (n((K, N)) / np.sqrt(K) / s).astype(np.float32),
        "rule": (n((N, U)) * 0.5 - 1.0).astype(np.float32),
        "offs": striped(np.random.permutation(T)[:S]),
        "la": striped(np.random.permutation(np.concatenate([np.arange(S), np.random.randint(0, S, U - S)]))),
        "ra": striped(np.random.permutation(np.concatenate([np.arange(S), np.random.randint(0, S, U - S)]))),
        "lb": striped(np.random.randint(0, V, W)),
        "rb": striped(np.random.randint(0, S, W)),
    }


def reference(x_words, x_scales, w1, rule, offs, la, ra, lb, rb):
    xq = unpack_weight(x_words, x_scales)[:, unstriped(offs)]
    y = mxq(f64(w1), 0, "e4m3").T @ xq
    cand = y[:, unstriped(la)] + y[:, unstriped(ra)] + f64(rule)
    top = cand.reshape(len(cand), -1, D).max(axis=2)
    ex = np.exp(cand - np.repeat(top, D, axis=1))
    ins = top + np.log(ex.reshape(len(ex), -1, D).sum(axis=2))
    cand2 = ins[:, unstriped(lb)] + y[:, unstriped(rb)]
    top2 = cand2.reshape(len(cand2), -1, D).max(axis=2)
    ey = np.exp(cand2 - np.repeat(top2, D, axis=1))
    return top2 + np.log(ey.reshape(len(ey), -1, D).sum(axis=2))

@@ -1,0 +1,163 @@
+from contextlib import ExitStack
+
+import concourse.mybir as mybir
+from concourse.masks import make_identity
+
+K, T, S, N, D, U, V, W = 512, 1024, 512, 256, 4, 1024, 256, 256
+FLOPS = 2 * K * N * S
+
+F32 = mybir.dt.float32
+BF16 = mybir.dt.bfloat16
+I32 = mybir.dt.int32
+U32 = mybir.dt.uint32
+U16 = mybir.dt.uint16
+U8 = mybir.dt.uint8
+FP8X4 = mybir.dt.float8_e4m3fn_x4
+ALU = mybir.AluOpType
+ACT = mybir.ActivationFunctionType
+AX = mybir.AxisListType
+
+P = 128
+BLOCKS = N // P
+CH = 512
+HALVES = U // CH
+SPARE = 16
+LA_ON_SCALAR = ()
+
+
+def tile_picked_ycky_ins_p_kernel(tc, x_words, x_scales, w1, rule, offs, la, ra, lb, rb, out):
+    nc = tc.nc
+    with ExitStack() as ctx:
+        keep = ctx.enter_context(tc.tile_pool(name="keep", bufs=1))
+        psum = ctx.enter_context(tc.psum_pool(name="psum", bufs=1))
+
+        offs_t = keep.tile([P, S // 16], U16, name="offs_t")
+        la_t = keep.tile([P, U // 16], U16, name="la_t")
+        ra_t = keep.tile([P, U // 16], U16, name="ra_t")
+        lb_t = keep.tile([P, W // 16], U16, name="lb_t")
+        rb_t = keep.tile([P, W // 16], U16, name="rb_t")
+        xw = keep.tile([P, T], U32, name="xw", align_bytes=64)
+        xs = keep.tile([P, T], U8, name="xs", align_bytes=64)
+        w_raw = [keep.tile([P, 4, P], F32, name=f"w_raw{b}") for b in range(BLOCKS)]
+        rule_t = [keep.tile([P, U], F32, name=f"rule{b}") for b in range(BLOCKS)]
+
+        nc.vector.memset(xs[:].bitcast(I32), 0)
+        for q in range(4):
+            nc.scalar.dma_start(xs[32 * q : 32 * q + 4, :].bitcast(I32), x_scales[0, 4 * q : 4 * q + 4, :].bitcast(I32))
+        w_view = w1.rearrange("(p j) n -> p j n", j=4)
+        nc.sync.dma_start(offs_t[:], offs)
+        nc.sync.dma_start(xw[:].bitcast(I32), x_words[0].rearrange("p n t -> p (n t)").bitcast(I32))
+        for b in range(BLOCKS):
+            nc.sync.dma_start(w_raw[b][:], w_view[:, :, b * P : (b + 1) * P])
+        nc.sync.dma_start(la_t[:], la)
+        nc.sync.dma_start(ra_t[:], ra)
+        nc.sync.dma_start(rule_t[0][:], rule[0:P, :])
+        nc.sync.dma_start(rule_t[1][:], rule[P : 2 * P, :])
+        nc.sync.dma_start(rb_t[:], rb)
+        nc.sync.dma_start(lb_t[:], lb)
+
+        y = [keep.tile([P, S + SPARE], F32, name=f"y{b}") for b in range(BLOCKS)]
+        ntop = [keep.tile([P, V + SPARE], F32, name=f"ntop{b}") for b in range(BLOCKS)]
+        ssum = [keep.tile([P, V + SPARE], F32, name=f"ssum{b}") for b in range(BLOCKS)]
+        ident = keep.tile([P, P], F32, name="ident")
+        for b in range(BLOCKS):
+            nc.gpsimd.memset(y[b][:, S:], 0.0)
+        make_identity(nc, ident[:])
+        for b in range(BLOCKS):
+            nc.gpsimd.memset(ntop[b][:, V:], 0.0)
+            nc.gpsimd.memset(ssum[b][:, V:], 0.0)
+
+        gs = keep.tile([P, S], U8, name="gs", align_bytes=64)
+        gw = keep.tile([P, S], U32, name="gw", align_bytes=64)
+        nc.vector.tensor_copy(gs[:], xs[:].indirect(offs_t[:]))
+        nc.vector.tensor_copy(gw[:], xw[:].indirect(offs_t[:]))
+
+        def product(b, pieces):
+            w_bf = keep.tile([P, P, 4], BF16, name=f"w_bf{b}", align_bytes=64)
+            nc.scalar.copy(
+                w_bf[:].rearrange("p (c i) t -> p c t i", i=4),
+                w_raw[b][:].rearrange("p t (c i) -> p c t i", i=4),
+            )
+            w_codes = keep.tile([P, P], U32, name=f"w_codes{b}", align_bytes=64)
+            w_scales = keep.tile([P, P], U8, name=f"w_scales{b}", align_bytes=64)
+            nc.vector.quantize_mx(
+                out=w_codes[:].bitcast(FP8X4), scales=w_scales[:], in_=w_bf[:].rearrange("p n t -> p (n t)")
+            )
+            for c0, c1, tag, copy in pieces:
+                acc = psum.tile([P, c1 - c0], F32, name="acc", tag=tag)
+                nc.tensor.matmul_mx(
+                    out=acc[:],
+                    lhsT=w_codes[:].bitcast(FP8X4),
+                    lhsT_scale=w_scales[:],
+                    rhs=gw[:, c0:c1].bitcast(FP8X4),
+                    rhs_scale=gs[:, c0:c1],
+                    start=True,
+                    stop=True,
+                )
+                copy(y[b][:, c0:c1], acc[:])
+
+        product(0, [(0, 256, "bank_a", nc.vector.tensor_copy), (256, 512, "bank_b", nc.scalar.copy)])
+        product(1, [(0, 512, "bank_c", nc.scalar.copy)])
+
+        total = keep.tile([P, BLOCKS, W // D], F32, name="total")
+        ntop2 = keep.tile([P, BLOCKS, W // D], F32, name="ntop2")
+
+        def first_level(b, h, sums):
+            c = b * HALVES + h
+            lcols = slice(h * CH // 16, (h + 1) * CH // 16)
+            rcols = slice(h * CH, (h + 1) * CH)
+            vcols = slice(h * P, (h + 1) * P)
+            right = keep.tile([P, CH], F32, name=f"right{c}")
+            nc.scalar.activation(right[:], y[b][:].indirect(ra_t[:, lcols]), ACT.Copy)
+            left = keep.tile([P, CH], F32, name=f"left{c}")
+            if c in LA_ON_SCALAR:
+                bare = keep.tile([P, CH], F32, name=f"bare{c}")
+                nc.scalar.activation(bare[:], y[b][:].indirect(la_t[:, lcols]), ACT.Copy)
+                nc.vector.tensor_tensor(left[:], bare[:], rule_t[b][:, rcols], ALU.add)
+            else:
+                nc.vector.tensor_tensor(left[:], y[b][:].indirect(la_t[:, lcols]), rule_t[b][:, rcols], ALU.add)
+            cand = keep.tile([P, P, D], F32, name=f"cand{c}")
+            nc.vector.tensor_tensor(cand[:].rearrange("p v d -> p (v d)"), left[:], right[:], ALU.add)
+            nc.vector.tensor_reduce(ntop[b][:, vcols], cand[:], AX.X, ALU.max, negate=True)
+            diff = psum.tile([P, D, P], F32, name="diff", tag=f"diff{c}")
+            for d in range(D):
+                nc.tensor.matmul(diff[:, d, :], cand[:, :, d], ident[:], start=(d == 0), stop=False, is_transpose=True)
+            for d in range(D):
+                nc.tensor.matmul(diff[:, d, :], ntop[b][:, vcols], ident[:], start=False, stop=(d == D - 1), is_transpose=True)
+            ex = keep.tile([P, D, P], F32, name=f"ex{c}")
+            nc.scalar.activation(ex[:], diff[:], ACT.Exp)
+            for d in range(D):
+                nc.tensor.matmul(sums[:, vcols], ex[:, d, :], ident[:], start=(d == 0), stop=(d == D - 1), is_transpose=True)
+            nc.scalar.copy(ssum[b][:, vcols], sums[:, vcols])
+
+        def second_level(b):
+            nshort = keep.tile([P, W], F32, name=f"nshort{b}")
+            nc.scalar.activation(nshort[:], y[b][:].indirect(rb_t[:]), ACT.Copy, scale=-1.0)
+            ncand = keep.tile([P, W // D, D], F32, name=f"ncand{b}")
+            nc.vector.tensor_tensor(
+                ncand[:].rearrange("p r d -> p (r d)"), ntop[b][:].indirect(lb_t[:]), nshort[:], ALU.add
+            )
+            nc.vector.tensor_reduce(ntop2[:, b, :], ncand[:], AX.X, ALU.min)
+            gap = keep.tile([P, W // D, D], F32, name=f"gap{b}")
+            nc.vector.tensor_tensor(
+                gap[:], ncand[:], ntop2[:, b, :].unsqueeze(2).to_broadcast([P, W // D, D]), ALU.subtract
+            )
+            ey = keep.tile([P, W], F32, name=f"ey{b}")
+            nc.scalar.activation(ey[:], gap[:].rearrange("p r d -> p (r d)"), ACT.Exp, scale=-1.0)
+            term = keep.tile([P, W // D, D], F32, name=f"term{b}")
+            nc.vector.tensor_tensor(
+                term[:].rearrange("p r d -> p (r d)"), ssum[b][:].indirect(lb_t[:]), ey[:], ALU.mult
+            )
+            nc.vector.tensor_reduce(total[:, b, :], term[:], AX.X, ALU.add)
+
+        for b in range(BLOCKS):
+            sums = psum.tile([P, V], F32, name="sums", tag=("bank_a", "bank_b")[b])
+            for h in range(HALVES):
+                first_level(b, h, sums)
+            second_level(b)
+
+        logs = keep.tile([P, BLOCKS, W // D], F32, name="logs")
+        nc.scalar.activation(logs[:], total[:], ACT.Ln)
+        res = keep.tile([P, BLOCKS, W // D], F32, name="res")
+        nc.vector.tensor_tensor(res[:], logs[:], ntop2[:], ALU.subtract)
+        nc.sync.dma_start(out.rearrange("(b p) r -> p b r", p=P), res[:])

@@ -18,11 +18,16 @@ ACT = mybir.ActivationFunctionType
 AX = mybir.AxisListType
 
 P = 128
+PACK = 4
+QUADRANT = 32
+PER_COLUMN = 16
 BLOCKS = N // P
-CH = 512
-HALVES = U // CH
+CHUNK = D * P
+PER_BLOCK = U // CHUNK
+CHUNKS = BLOCKS * PER_BLOCK
+LAST = CHUNKS - 1
+R = W // D
 SPARE = 16
-LA_ON_SCALAR = ()
 
 
 def tile_picked_ycky_ins_p_kernel(tc, x_words, x_scales, w1, rule, offs, la, ra, lb, rb, out):
@@ -31,133 +36,185 @@ def tile_picked_ycky_ins_p_kernel(tc, x_words, x_scales, w1, rule, offs, la, ra,
         keep = ctx.enter_context(tc.tile_pool(name="keep", bufs=1))
         psum = ctx.enter_context(tc.psum_pool(name="psum", bufs=1))
 
-        offs_t = keep.tile([P, S // 16], U16, name="offs_t")
-        la_t = keep.tile([P, U // 16], U16, name="la_t")
-        ra_t = keep.tile([P, U // 16], U16, name="ra_t")
-        lb_t = keep.tile([P, W // 16], U16, name="lb_t")
-        rb_t = keep.tile([P, W // 16], U16, name="rb_t")
-        xw = keep.tile([P, T], U32, name="xw", align_bytes=64)
-        xs = keep.tile([P, T], U8, name="xs", align_bytes=64)
-        w_raw = [keep.tile([P, 4, P], F32, name=f"w_raw{b}") for b in range(BLOCKS)]
+        offs_t = keep.tile([P, S // PER_COLUMN], U16, name="offs_t")
+        la_t = keep.tile([P, U // PER_COLUMN], U16, name="la_t")
+        ra_t = keep.tile([P, U // PER_COLUMN], U16, name="ra_t")
+        lb_t = keep.tile([P, W // PER_COLUMN], U16, name="lb_t")
+        rb_t = keep.tile([P, W // PER_COLUMN], U16, name="rb_t")
+        words = keep.tile([P, T], U32, name="words", align_bytes=64)
+        scales = keep.tile([P, T], U8, name="scales", align_bytes=64)
+        w_raw = [keep.tile([P, PACK, P], F32, name=f"w_raw{b}") for b in range(BLOCKS)]
         rule_t = [keep.tile([P, U], F32, name=f"rule{b}") for b in range(BLOCKS)]
 
-        nc.vector.memset(xs[:].bitcast(I32), 0)
-        for q in range(4):
-            nc.scalar.dma_start(xs[32 * q : 32 * q + 4, :].bitcast(I32), x_scales[0, 4 * q : 4 * q + 4, :].bitcast(I32))
-        w_view = w1.rearrange("(p j) n -> p j n", j=4)
+        def load_scale_rows(queue, q):
+            rows = x_scales[0, PACK * q : PACK * (q + 1), :].bitcast(I32)
+            queue.dma_start(
+                scales[QUADRANT * q : QUADRANT * (q + 1), :].bitcast(I32),
+                rows.unsqueeze(0).to_broadcast([QUADRANT // PACK, PACK, T // 4]),
+            )
+
+        w_view = w1.rearrange("(p j) n -> p j n", j=PACK)
+        for q in (2, 3):
+            load_scale_rows(nc.sync, q)
         nc.sync.dma_start(offs_t[:], offs)
-        nc.sync.dma_start(xw[:].bitcast(I32), x_words[0].rearrange("p n t -> p (n t)").bitcast(I32))
+        nc.sync.dma_start(words[:].bitcast(I32), x_words[0].rearrange("p n t -> p (n t)").bitcast(I32))
         for b in range(BLOCKS):
             nc.sync.dma_start(w_raw[b][:], w_view[:, :, b * P : (b + 1) * P])
-        nc.sync.dma_start(la_t[:], la)
         nc.sync.dma_start(ra_t[:], ra)
-        nc.sync.dma_start(rule_t[0][:], rule[0:P, :])
-        nc.sync.dma_start(rule_t[1][:], rule[P : 2 * P, :])
+        nc.sync.dma_start(la_t[:], la)
+        for b in range(BLOCKS):
+            nc.sync.dma_start(rule_t[b][:], rule[b * P : (b + 1) * P, :])
         nc.sync.dma_start(rb_t[:], rb)
         nc.sync.dma_start(lb_t[:], lb)
+        for q in (0, 1):
+            load_scale_rows(nc.scalar, q)
 
         y = [keep.tile([P, S + SPARE], F32, name=f"y{b}") for b in range(BLOCKS)]
-        ntop = [keep.tile([P, V + SPARE], F32, name=f"ntop{b}") for b in range(BLOCKS)]
-        ssum = [keep.tile([P, V + SPARE], F32, name=f"ssum{b}") for b in range(BLOCKS)]
+        neg_top = [keep.tile([P, V + SPARE], F32, name=f"neg_top{b}") for b in range(BLOCKS)]
+        mass = [keep.tile([P, V + SPARE], F32, name=f"mass{b}") for b in range(BLOCKS)]
         ident = keep.tile([P, P], F32, name="ident")
         for b in range(BLOCKS):
             nc.gpsimd.memset(y[b][:, S:], 0.0)
         make_identity(nc, ident[:])
         for b in range(BLOCKS):
-            nc.gpsimd.memset(ntop[b][:, V:], 0.0)
-            nc.gpsimd.memset(ssum[b][:, V:], 0.0)
+            nc.gpsimd.memset(neg_top[b][:, V:], 0.0)
+            nc.gpsimd.memset(mass[b][:, V:], 0.0)
 
-        gs = keep.tile([P, S], U8, name="gs", align_bytes=64)
-        gw = keep.tile([P, S], U32, name="gw", align_bytes=64)
-        nc.vector.tensor_copy(gs[:], xs[:].indirect(offs_t[:]))
-        nc.vector.tensor_copy(gw[:], xw[:].indirect(offs_t[:]))
+        picked_scales = keep.tile([P, S], U8, name="picked_scales", align_bytes=64)
+        picked_words = keep.tile([P, S], U32, name="picked_words", align_bytes=64)
+        nc.vector.tensor_copy(picked_scales[:], scales[:].indirect(offs_t[:]))
+        nc.vector.tensor_copy(picked_words[:], words[:].indirect(offs_t[:]))
 
         def product(b, pieces):
-            w_bf = keep.tile([P, P, 4], BF16, name=f"w_bf{b}", align_bytes=64)
+            w_bf = keep.tile([P, P, PACK], BF16, name=f"w_bf{b}", align_bytes=64)
             nc.scalar.copy(
-                w_bf[:].rearrange("p (c i) t -> p c t i", i=4),
-                w_raw[b][:].rearrange("p t (c i) -> p c t i", i=4),
+                w_bf[:].rearrange("p (c i) j -> p c j i", i=4),
+                w_raw[b][:].rearrange("p j (c i) -> p c j i", i=4),
             )
             w_codes = keep.tile([P, P], U32, name=f"w_codes{b}", align_bytes=64)
             w_scales = keep.tile([P, P], U8, name=f"w_scales{b}", align_bytes=64)
             nc.vector.quantize_mx(
-                out=w_codes[:].bitcast(FP8X4), scales=w_scales[:], in_=w_bf[:].rearrange("p n t -> p (n t)")
+                out=w_codes[:].bitcast(FP8X4), scales=w_scales[:], in_=w_bf[:].rearrange("p n j -> p (n j)")
             )
-            for c0, c1, tag, copy in pieces:
-                acc = psum.tile([P, c1 - c0], F32, name="acc", tag=tag)
+            for c0, c1, bank, copy_out in pieces:
+                acc = psum.tile([P, c1 - c0], F32, name="acc", tag=bank)
                 nc.tensor.matmul_mx(
                     out=acc[:],
                     lhsT=w_codes[:].bitcast(FP8X4),
                     lhsT_scale=w_scales[:],
-                    rhs=gw[:, c0:c1].bitcast(FP8X4),
-                    rhs_scale=gs[:, c0:c1],
+                    rhs=picked_words[:, c0:c1].bitcast(FP8X4),
+                    rhs_scale=picked_scales[:, c0:c1],
                     start=True,
                     stop=True,
                 )
-                copy(y[b][:, c0:c1], acc[:])
+                copy_out(y[b][:, c0:c1], acc[:])
 
-        product(0, [(0, 256, "bank_a", nc.vector.tensor_copy), (256, 512, "bank_b", nc.scalar.copy)])
-        product(1, [(0, 512, "bank_c", nc.scalar.copy)])
+        banks = ("bank_a", "bank_b", "bank_c")
+        product(0, [(0, S // 2, banks[0], nc.vector.tensor_copy), (S // 2, S, banks[1], nc.scalar.copy)])
+        product(1, [(0, S, banks[2], nc.vector.tensor_copy)])
 
-        total = keep.tile([P, BLOCKS, W // D], F32, name="total")
-        ntop2 = keep.tile([P, BLOCKS, W // D], F32, name="ntop2")
+        def groups(c):
+            return slice((c % PER_BLOCK) * P, (c % PER_BLOCK + 1) * P)
 
-        def first_level(b, h, sums):
-            c = b * HALVES + h
-            lcols = slice(h * CH // 16, (h + 1) * CH // 16)
-            rcols = slice(h * CH, (h + 1) * CH)
-            vcols = slice(h * P, (h + 1) * P)
-            right = keep.tile([P, CH], F32, name=f"right{c}")
-            nc.scalar.activation(right[:], y[b][:].indirect(ra_t[:, lcols]), ACT.Copy)
-            left = keep.tile([P, CH], F32, name=f"left{c}")
-            if c in LA_ON_SCALAR:
-                bare = keep.tile([P, CH], F32, name=f"bare{c}")
-                nc.scalar.activation(bare[:], y[b][:].indirect(la_t[:, lcols]), ACT.Copy)
-                nc.vector.tensor_tensor(left[:], bare[:], rule_t[b][:, rcols], ALU.add)
+        def transpose_add(dst, src, start, stop):
+            nc.tensor.matmul(dst, src, ident[:], start=start, stop=stop, is_transpose=True)
+
+        shifted = []
+        for c in range(CHUNKS):
+            b, h = divmod(c, PER_BLOCK)
+            entries = slice(h * CHUNK // PER_COLUMN, (h + 1) * CHUNK // PER_COLUMN)
+            rule_c = rule_t[b][:, h * CHUNK : (h + 1) * CHUNK]
+            right = keep.tile([P, CHUNK], F32, name=f"right{c}")
+            with_rule = keep.tile([P, CHUNK], F32, name=f"with_rule{c}")
+            nc.scalar.activation(right[:], y[b][:].indirect(ra_t[:, entries]), ACT.Copy)
+            if b == 0:
+                nc.vector.tensor_tensor(with_rule[:], y[b][:].indirect(la_t[:, entries]), rule_c, ALU.add)
+                other = right
             else:
-                nc.vector.tensor_tensor(left[:], y[b][:].indirect(la_t[:, lcols]), rule_t[b][:, rcols], ALU.add)
-            cand = keep.tile([P, P, D], F32, name=f"cand{c}")
-            nc.vector.tensor_tensor(cand[:].rearrange("p v d -> p (v d)"), left[:], right[:], ALU.add)
-            nc.vector.tensor_reduce(ntop[b][:, vcols], cand[:], AX.X, ALU.max, negate=True)
-            diff = psum.tile([P, D, P], F32, name="diff", tag=f"diff{c}")
-            for d in range(D):
-                nc.tensor.matmul(diff[:, d, :], cand[:, :, d], ident[:], start=(d == 0), stop=False, is_transpose=True)
-            for d in range(D):
-                nc.tensor.matmul(diff[:, d, :], ntop[b][:, vcols], ident[:], start=False, stop=(d == D - 1), is_transpose=True)
-            ex = keep.tile([P, D, P], F32, name=f"ex{c}")
-            nc.scalar.activation(ex[:], diff[:], ACT.Exp)
-            for d in range(D):
-                nc.tensor.matmul(sums[:, vcols], ex[:, d, :], ident[:], start=(d == 0), stop=(d == D - 1), is_transpose=True)
-            nc.scalar.copy(ssum[b][:, vcols], sums[:, vcols])
+                other = keep.tile([P, CHUNK], F32, name=f"left{c}")
+                nc.scalar.activation(other[:], y[b][:].indirect(la_t[:, entries]), ACT.Copy)
+                nc.vector.tensor_tensor(with_rule[:], right[:], rule_c, ALU.add)
 
-        def second_level(b):
-            nshort = keep.tile([P, W], F32, name=f"nshort{b}")
-            nc.scalar.activation(nshort[:], y[b][:].indirect(rb_t[:]), ACT.Copy, scale=-1.0)
-            ncand = keep.tile([P, W // D, D], F32, name=f"ncand{b}")
-            nc.vector.tensor_tensor(
-                ncand[:].rearrange("p r d -> p (r d)"), ntop[b][:].indirect(lb_t[:]), nshort[:], ALU.add
+            cand = keep.tile([P, CHUNK], F32, name=f"cand{c}")
+            neg_top_c = neg_top[b][:, groups(c)]
+            if c == LAST:
+                by_group = cand[:].rearrange("p (v d) -> p v d", d=D)
+                nc.vector.tensor_tensor(cand[:], with_rule[:], other[:], ALU.add)
+                nc.vector.tensor_reduce(neg_top_c, by_group, AX.X, ALU.max, negate=True)
+                diff = keep.tile([P, P, D], F32, name="last_diff")
+                nc.vector.tensor_tensor(diff[:], by_group, neg_top_c.unsqueeze(2).to_broadcast([P, P, D]), ALU.add)
+            else:
+                halves = cand[:].rearrange("p (hi v lo) -> p v hi lo", hi=2, lo=2)
+                nc.vector.tensor_tensor(
+                    halves,
+                    with_rule[:].rearrange("p (v hi lo) -> p v hi lo", hi=2, lo=2),
+                    other[:].rearrange("p (v hi lo) -> p v hi lo", hi=2, lo=2),
+                    ALU.add,
+                )
+                nc.vector.tensor_reduce(neg_top_c, halves, AX.XY, ALU.max, negate=True)
+                diff = psum.tile([P, D, P], F32, name="diff", tag=f"diff{c}")
+                for d in range(D):
+                    transpose_add(diff[:, d, :], halves[:, :, d // 2, d % 2], d == 0, False)
+                for d in range(D):
+                    transpose_add(diff[:, d, :], neg_top_c, False, d == D - 1)
+            shifted.append(diff)
+
+        neg_short = []
+        for b in range(BLOCKS):
+            neg_short.append(keep.tile([P, W], F32, name=f"neg_short{b}"))
+            nc.scalar.activation(neg_short[b][:], y[b][:].indirect(rb_t[:]), ACT.Copy, scale=-1.0)
+
+        first_block_ex = keep.tile([P, PER_BLOCK, CHUNK], F32, name="first_block_ex", tag=f"cand{PER_BLOCK}")
+        ex = []
+        for c in range(CHUNKS):
+            ex.append(first_block_ex[:, c, :] if c < PER_BLOCK else keep.tile([P, CHUNK], F32, name=f"ex{c}")[:])
+            nc.scalar.activation(ex[c], shifted[c][:].rearrange("p a b -> p (a b)"), ACT.Exp)
+
+        def look_up_long(dst, window, plain, op, b, name):
+            if b == 0:
+                fetched = keep.tile([P, W], F32, name=name)
+                nc.scalar.activation(fetched[:], window[:].indirect(lb_t[:]), ACT.Copy)
+                nc.vector.tensor_tensor(dst, fetched[:], plain, op)
+            else:
+                nc.vector.tensor_tensor(dst, window[:].indirect(lb_t[:]), plain, op)
+
+        neg_both = []
+        for b in range(BLOCKS):
+            neg_both.append(keep.tile([P, R, D], F32, name=f"neg_both{b}"))
+            look_up_long(
+                neg_both[b][:].rearrange("p r d -> p (r d)"), neg_top[b], neg_short[b][:], ALU.add, b, "neg_long"
             )
-            nc.vector.tensor_reduce(ntop2[:, b, :], ncand[:], AX.X, ALU.min)
-            gap = keep.tile([P, W // D, D], F32, name=f"gap{b}")
+
+        for c in range(CHUNKS):
+            b = c // PER_BLOCK
+            mass_c = mass[b][:, groups(c)]
+            if c == LAST:
+                nc.vector.tensor_reduce(mass_c, ex[c].rearrange("p (v d) -> p v d", d=D), AX.X, ALU.add)
+            else:
+                summed = psum.tile([P, P], F32, name="summed", tag=banks[c])
+                for d in range(D):
+                    transpose_add(summed[:], ex[c][:, d * P : (d + 1) * P], d == 0, d == D - 1)
+                copy_out = nc.scalar.copy if b == 0 else nc.vector.tensor_copy
+                copy_out(mass_c, summed[:])
+
+        neg_peak = keep.tile([P, BLOCKS, R], F32, name="neg_peak")
+        total = keep.tile([P, BLOCKS, R], F32, name="total")
+        ey = []
+        for b in range(BLOCKS):
+            nc.vector.tensor_reduce(neg_peak[:, b, :], neg_both[b][:], AX.X, ALU.min)
+            gap = keep.tile([P, R, D], F32, name=f"gap{b}")
             nc.vector.tensor_tensor(
-                gap[:], ncand[:], ntop2[:, b, :].unsqueeze(2).to_broadcast([P, W // D, D]), ALU.subtract
+                gap[:], neg_both[b][:], neg_peak[:, b, :].unsqueeze(2).to_broadcast([P, R, D]), ALU.subtract
             )
-            ey = keep.tile([P, W], F32, name=f"ey{b}")
-            nc.scalar.activation(ey[:], gap[:].rearrange("p r d -> p (r d)"), ACT.Exp, scale=-1.0)
-            term = keep.tile([P, W // D, D], F32, name=f"term{b}")
-            nc.vector.tensor_tensor(
-                term[:].rearrange("p r d -> p (r d)"), ssum[b][:].indirect(lb_t[:]), ey[:], ALU.mult
-            )
+            ey.append(keep.tile([P, W], F32, name=f"ey{b}"))
+            nc.scalar.activation(ey[b][:], gap[:].rearrange("p r d -> p (r d)"), ACT.Exp, scale=-1.0)
+        for b in range(BLOCKS):
+            term = keep.tile([P, R, D], F32, name=f"term{b}")
+            look_up_long(term[:].rearrange("p r d -> p (r d)"), mass[b], ey[b][:], ALU.mult, b, "long_mass")
             nc.vector.tensor_reduce(total[:, b, :], term[:], AX.X, ALU.add)
 
-        for b in range(BLOCKS):
-            sums = psum.tile([P, V], F32, name="sums", tag=("bank_a", "bank_b")[b])
-            for h in range(HALVES):
-                first_level(b, h, sums)
-            second_level(b)
-
-        logs = keep.tile([P, BLOCKS, W // D], F32, name="logs")
+        logs = keep.tile([P, BLOCKS, R], F32, name="logs")
         nc.scalar.activation(logs[:], total[:], ACT.Ln)
-        res = keep.tile([P, BLOCKS, W // D], F32, name="res")
-        nc.vector.tensor_tensor(res[:], logs[:], ntop2[:], ALU.subtract)
-        nc.sync.dma_start(out.rearrange("(b p) r -> p b r", p=P), res[:])
+        result = keep.tile([P, BLOCKS, R], F32, name="result")
+        nc.vector.tensor_tensor(result[:], logs[:], neg_peak[:], ALU.subtract)
+        nc.sync.dma_start(out.rearrange("(b p) r -> p b r", p=P), result[:])

@@ -25,7 +25,7 @@ BLOCKS = N // P
 CHUNK = D * P
 PER_BLOCK = U // CHUNK
 CHUNKS = BLOCKS * PER_BLOCK
-LAST = CHUNKS - 1
+SCALAR_ONLY = 2
 R = W // D
 SPARE = 16
 
@@ -109,9 +109,9 @@ def tile_picked_ycky_ins_p_kernel(tc, x_words, x_scales, w1, rule, offs, la, ra,
                 )
                 copy_out(y[b][:, c0:c1], acc[:])
 
-        banks = ("bank_a", "bank_b", "bank_c")
+        banks = ("bank_a", "bank_b", "bank_c", "bank_d")
         product(0, [(0, S // 2, banks[0], nc.vector.tensor_copy), (S // 2, S, banks[1], nc.scalar.copy)])
-        product(1, [(0, S, banks[2], nc.vector.tensor_copy)])
+        product(1, [(0, S, banks[2], nc.scalar.copy)])
 
         def groups(c):
             return slice((c % PER_BLOCK) * P, (c % PER_BLOCK + 1) * P)
@@ -127,75 +127,52 @@ def tile_picked_ycky_ins_p_kernel(tc, x_words, x_scales, w1, rule, offs, la, ra,
             right = keep.tile([P, CHUNK], F32, name=f"right{c}")
             with_rule = keep.tile([P, CHUNK], F32, name=f"with_rule{c}")
             nc.scalar.activation(right[:], y[b][:].indirect(ra_t[:, entries]), ACT.Copy)
-            if b == 0:
-                nc.vector.tensor_tensor(with_rule[:], y[b][:].indirect(la_t[:, entries]), rule_c, ALU.add)
-                other = right
-            else:
-                other = keep.tile([P, CHUNK], F32, name=f"left{c}")
+            if c == SCALAR_ONLY:
+                other = keep.tile([P, CHUNK], F32, name="left")
                 nc.scalar.activation(other[:], y[b][:].indirect(la_t[:, entries]), ACT.Copy)
                 nc.vector.tensor_tensor(with_rule[:], right[:], rule_c, ALU.add)
+            else:
+                nc.vector.tensor_tensor(with_rule[:], y[b][:].indirect(la_t[:, entries]), rule_c, ALU.add)
+                other = right
 
             cand = keep.tile([P, CHUNK], F32, name=f"cand{c}")
             neg_top_c = neg_top[b][:, groups(c)]
-            if c == LAST:
-                by_group = cand[:].rearrange("p (v d) -> p v d", d=D)
-                nc.vector.tensor_tensor(cand[:], with_rule[:], other[:], ALU.add)
-                nc.vector.tensor_reduce(neg_top_c, by_group, AX.X, ALU.max, negate=True)
-                diff = keep.tile([P, P, D], F32, name="last_diff")
-                nc.vector.tensor_tensor(diff[:], by_group, neg_top_c.unsqueeze(2).to_broadcast([P, P, D]), ALU.add)
-            else:
-                halves = cand[:].rearrange("p (hi v lo) -> p v hi lo", hi=2, lo=2)
-                nc.vector.tensor_tensor(
-                    halves,
-                    with_rule[:].rearrange("p (v hi lo) -> p v hi lo", hi=2, lo=2),
-                    other[:].rearrange("p (v hi lo) -> p v hi lo", hi=2, lo=2),
-                    ALU.add,
-                )
-                nc.vector.tensor_reduce(neg_top_c, halves, AX.XY, ALU.max, negate=True)
-                diff = psum.tile([P, D, P], F32, name="diff", tag=f"diff{c}")
-                for d in range(D):
-                    transpose_add(diff[:, d, :], halves[:, :, d // 2, d % 2], d == 0, False)
-                for d in range(D):
-                    transpose_add(diff[:, d, :], neg_top_c, False, d == D - 1)
+            halves = cand[:].rearrange("p (hi v lo) -> p v hi lo", hi=2, lo=2)
+            nc.vector.tensor_tensor(
+                halves,
+                with_rule[:].rearrange("p (v hi lo) -> p v hi lo", hi=2, lo=2),
+                other[:].rearrange("p (v hi lo) -> p v hi lo", hi=2, lo=2),
+                ALU.add,
+            )
+            nc.vector.tensor_reduce(neg_top_c, halves, AX.XY, ALU.max, negate=True)
+            diff = psum.tile([P, D, P], F32, name="diff", tag=f"diff{c}")
+            for d in range(D):
+                transpose_add(diff[:, d, :], halves[:, :, d // 2, d % 2], d == 0, False)
+            for d in range(D):
+                transpose_add(diff[:, d, :], neg_top_c, False, d == D - 1)
             shifted.append(diff)
 
-        neg_short = []
+        neg_short = keep.tile([P, BLOCKS, W], F32, name="neg_short", tag=f"with_rule{SCALAR_ONLY}")
         for b in range(BLOCKS):
-            neg_short.append(keep.tile([P, W], F32, name=f"neg_short{b}"))
-            nc.scalar.activation(neg_short[b][:], y[b][:].indirect(rb_t[:]), ACT.Copy, scale=-1.0)
+            nc.scalar.activation(neg_short[:, b, :], y[b][:].indirect(rb_t[:]), ACT.Copy, scale=-1.0)
 
-        first_block_ex = keep.tile([P, PER_BLOCK, CHUNK], F32, name="first_block_ex", tag=f"cand{PER_BLOCK}")
         ex = []
         for c in range(CHUNKS):
-            ex.append(first_block_ex[:, c, :] if c < PER_BLOCK else keep.tile([P, CHUNK], F32, name=f"ex{c}")[:])
-            nc.scalar.activation(ex[c], shifted[c][:].rearrange("p a b -> p (a b)"), ACT.Exp)
-
-        def look_up_long(dst, window, plain, op, b, name):
-            if b == 0:
-                fetched = keep.tile([P, W], F32, name=name)
-                nc.scalar.activation(fetched[:], window[:].indirect(lb_t[:]), ACT.Copy)
-                nc.vector.tensor_tensor(dst, fetched[:], plain, op)
-            else:
-                nc.vector.tensor_tensor(dst, window[:].indirect(lb_t[:]), plain, op)
+            ex.append(keep.tile([P, D, P], F32, name=f"ex{c}"))
+            nc.scalar.activation(ex[c][:], shifted[c][:], ACT.Exp)
 
         neg_both = []
         for b in range(BLOCKS):
             neg_both.append(keep.tile([P, R, D], F32, name=f"neg_both{b}"))
-            look_up_long(
-                neg_both[b][:].rearrange("p r d -> p (r d)"), neg_top[b], neg_short[b][:], ALU.add, b, "neg_long"
+            nc.vector.tensor_tensor(
+                neg_both[b][:].rearrange("p r d -> p (r d)"), neg_top[b][:].indirect(lb_t[:]), neg_short[:, b, :], ALU.add
             )
 
         for c in range(CHUNKS):
-            b = c // PER_BLOCK
-            mass_c = mass[b][:, groups(c)]
-            if c == LAST:
-                nc.vector.tensor_reduce(mass_c, ex[c].rearrange("p (v d) -> p v d", d=D), AX.X, ALU.add)
-            else:
-                summed = psum.tile([P, P], F32, name="summed", tag=banks[c])
-                for d in range(D):
-                    transpose_add(summed[:], ex[c][:, d * P : (d + 1) * P], d == 0, d == D - 1)
-                copy_out = nc.scalar.copy if b == 0 else nc.vector.tensor_copy
-                copy_out(mass_c, summed[:])
+            summed = psum.tile([P, P], F32, name="summed", tag=banks[c])
+            for d in range(D):
+                transpose_add(summed[:], ex[c][:, d, :], d == 0, d == D - 1)
+            nc.scalar.copy(mass[c // PER_BLOCK][:, groups(c)], summed[:])
 
         neg_peak = keep.tile([P, BLOCKS, R], F32, name="neg_peak")
         total = keep.tile([P, BLOCKS, R], F32, name="total")
@@ -210,7 +187,9 @@ def tile_picked_ycky_ins_p_kernel(tc, x_words, x_scales, w1, rule, offs, la, ra,
             nc.scalar.activation(ey[b][:], gap[:].rearrange("p r d -> p (r d)"), ACT.Exp, scale=-1.0)
         for b in range(BLOCKS):
             term = keep.tile([P, R, D], F32, name=f"term{b}")
-            look_up_long(term[:].rearrange("p r d -> p (r d)"), mass[b], ey[b][:], ALU.mult, b, "long_mass")
+            nc.vector.tensor_tensor(
+                term[:].rearrange("p r d -> p (r d)"), mass[b][:].indirect(lb_t[:]), ey[b][:], ALU.mult
+            )
             nc.vector.tensor_reduce(total[:, b, :], term[:], AX.X, ALU.add)
 
         logs = keep.tile([P, BLOCKS, R], F32, name="logs")

from contextlib import ExitStack

import concourse.mybir as mybir
from concourse.masks import make_identity

K, T, S, N, D, U, V, W = 512, 1024, 512, 256, 4, 1024, 256, 256
FLOPS = 2 * K * N * S

F32 = mybir.dt.float32
BF16 = mybir.dt.bfloat16
I32 = mybir.dt.int32
U32 = mybir.dt.uint32
U16 = mybir.dt.uint16
U8 = mybir.dt.uint8
FP8X4 = mybir.dt.float8_e4m3fn_x4
ALU = mybir.AluOpType
ACT = mybir.ActivationFunctionType
AX = mybir.AxisListType

P = 128
PACK = 4
QUADRANT = 32
PER_COLUMN = 16
BLOCKS = N // P
CHUNK = D * P
PER_BLOCK = U // CHUNK
CHUNKS = BLOCKS * PER_BLOCK
SCALAR_ONLY = 2
R = W // D
SPARE = 16


def tile_picked_ycky_ins_p_kernel(tc, x_words, x_scales, w1, rule, offs, la, ra, lb, rb, out):
    nc = tc.nc
    with ExitStack() as ctx:
        keep = ctx.enter_context(tc.tile_pool(name="keep", bufs=1))
        psum = ctx.enter_context(tc.psum_pool(name="psum", bufs=1))

        offs_t = keep.tile([P, S // PER_COLUMN], U16, name="offs_t")
        la_t = keep.tile([P, U // PER_COLUMN], U16, name="la_t")
        ra_t = keep.tile([P, U // PER_COLUMN], U16, name="ra_t")
        lb_t = keep.tile([P, W // PER_COLUMN], U16, name="lb_t")
        rb_t = keep.tile([P, W // PER_COLUMN], U16, name="rb_t")
        words = keep.tile([P, T], U32, name="words", align_bytes=64)
        scales = keep.tile([P, T], U8, name="scales", align_bytes=64)
        w_raw = [keep.tile([P, PACK, P], F32, name=f"w_raw{b}") for b in range(BLOCKS)]
        rule_t = [keep.tile([P, U], F32, name=f"rule{b}") for b in range(BLOCKS)]

        def load_scale_rows(queue, q):
            rows = x_scales[0, PACK * q : PACK * (q + 1), :].bitcast(I32)
            queue.dma_start(
                scales[QUADRANT * q : QUADRANT * (q + 1), :].bitcast(I32),
                rows.unsqueeze(0).to_broadcast([QUADRANT // PACK, PACK, T // 4]),
            )

        w_view = w1.rearrange("(p j) n -> p j n", j=PACK)
        for q in (2, 3):
            load_scale_rows(nc.sync, q)
        nc.sync.dma_start(offs_t[:], offs)
        nc.sync.dma_start(words[:].bitcast(I32), x_words[0].rearrange("p n t -> p (n t)").bitcast(I32))
        for b in range(BLOCKS):
            nc.sync.dma_start(w_raw[b][:], w_view[:, :, b * P : (b + 1) * P])
        nc.sync.dma_start(ra_t[:], ra)
        nc.sync.dma_start(la_t[:], la)
        for b in range(BLOCKS):
            nc.sync.dma_start(rule_t[b][:], rule[b * P : (b + 1) * P, :])
        nc.sync.dma_start(rb_t[:], rb)
        nc.sync.dma_start(lb_t[:], lb)
        for q in (0, 1):
            load_scale_rows(nc.scalar, q)

        y = [keep.tile([P, S + SPARE], F32, name=f"y{b}") for b in range(BLOCKS)]
        neg_top = [keep.tile([P, V + SPARE], F32, name=f"neg_top{b}") for b in range(BLOCKS)]
        mass = [keep.tile([P, V + SPARE], F32, name=f"mass{b}") for b in range(BLOCKS)]
        ident = keep.tile([P, P], F32, name="ident")
        for b in range(BLOCKS):
            nc.gpsimd.memset(y[b][:, S:], 0.0)
        make_identity(nc, ident[:])
        for b in range(BLOCKS):
            nc.gpsimd.memset(neg_top[b][:, V:], 0.0)
            nc.gpsimd.memset(mass[b][:, V:], 0.0)

        picked_scales = keep.tile([P, S], U8, name="picked_scales", align_bytes=64)
        picked_words = keep.tile([P, S], U32, name="picked_words", align_bytes=64)
        nc.vector.tensor_copy(picked_scales[:], scales[:].indirect(offs_t[:]))
        nc.vector.tensor_copy(picked_words[:], words[:].indirect(offs_t[:]))

        def product(b, pieces):
            w_bf = keep.tile([P, P, PACK], BF16, name=f"w_bf{b}", align_bytes=64)
            nc.scalar.copy(
                w_bf[:].rearrange("p (c i) j -> p c j i", i=4),
                w_raw[b][:].rearrange("p j (c i) -> p c j i", i=4),
            )
            w_codes = keep.tile([P, P], U32, name=f"w_codes{b}", align_bytes=64)
            w_scales = keep.tile([P, P], U8, name=f"w_scales{b}", align_bytes=64)
            nc.vector.quantize_mx(
                out=w_codes[:].bitcast(FP8X4), scales=w_scales[:], in_=w_bf[:].rearrange("p n j -> p (n j)")
            )
            for c0, c1, bank, copy_out in pieces:
                acc = psum.tile([P, c1 - c0], F32, name="acc", tag=bank)
                nc.tensor.matmul_mx(
                    out=acc[:],
                    lhsT=w_codes[:].bitcast(FP8X4),
                    lhsT_scale=w_scales[:],
                    rhs=picked_words[:, c0:c1].bitcast(FP8X4),
                    rhs_scale=picked_scales[:, c0:c1],
                    start=True,
                    stop=True,
                )
                copy_out(y[b][:, c0:c1], acc[:])

        banks = ("bank_a", "bank_b", "bank_c", "bank_d")
        product(0, [(0, S // 2, banks[0], nc.vector.tensor_copy), (S // 2, S, banks[1], nc.scalar.copy)])
        product(1, [(0, S, banks[2], nc.scalar.copy)])

        def groups(c):
            return slice((c % PER_BLOCK) * P, (c % PER_BLOCK + 1) * P)

        def transpose_add(dst, src, start, stop):
            nc.tensor.matmul(dst, src, ident[:], start=start, stop=stop, is_transpose=True)

        shifted = []
        for c in range(CHUNKS):
            b, h = divmod(c, PER_BLOCK)
            entries = slice(h * CHUNK // PER_COLUMN, (h + 1) * CHUNK // PER_COLUMN)
            rule_c = rule_t[b][:, h * CHUNK : (h + 1) * CHUNK]
            right = keep.tile([P, CHUNK], F32, name=f"right{c}")
            with_rule = keep.tile([P, CHUNK], F32, name=f"with_rule{c}")
            nc.scalar.activation(right[:], y[b][:].indirect(ra_t[:, entries]), ACT.Copy)
            if c == SCALAR_ONLY:
                other = keep.tile([P, CHUNK], F32, name="left")
                nc.scalar.activation(other[:], y[b][:].indirect(la_t[:, entries]), ACT.Copy)
                nc.vector.tensor_tensor(with_rule[:], right[:], rule_c, ALU.add)
            else:
                nc.vector.tensor_tensor(with_rule[:], y[b][:].indirect(la_t[:, entries]), rule_c, ALU.add)
                other = right

            cand = keep.tile([P, CHUNK], F32, name=f"cand{c}")
            neg_top_c = neg_top[b][:, groups(c)]
            halves = cand[:].rearrange("p (hi v lo) -> p v hi lo", hi=2, lo=2)
            nc.vector.tensor_tensor(
                halves,
                with_rule[:].rearrange("p (v hi lo) -> p v hi lo", hi=2, lo=2),
                other[:].rearrange("p (v hi lo) -> p v hi lo", hi=2, lo=2),
                ALU.add,
            )
            nc.vector.tensor_reduce(neg_top_c, halves, AX.XY, ALU.max, negate=True)
            diff = psum.tile([P, D, P], F32, name="diff", tag=f"diff{c}")
            for d in range(D):
                transpose_add(diff[:, d, :], halves[:, :, d // 2, d % 2], d == 0, False)
            for d in range(D):
                transpose_add(diff[:, d, :], neg_top_c, False, d == D - 1)
            shifted.append(diff)

        neg_short = keep.tile([P, BLOCKS, W], F32, name="neg_short", tag=f"with_rule{SCALAR_ONLY}")
        for b in range(BLOCKS):
            nc.scalar.activation(neg_short[:, b, :], y[b][:].indirect(rb_t[:]), ACT.Copy, scale=-1.0)

        ex = []
        for c in range(CHUNKS):
            ex.append(keep.tile([P, D, P], F32, name=f"ex{c}"))
            nc.scalar.activation(ex[c][:], shifted[c][:], ACT.Exp)

        neg_both = []
        for b in range(BLOCKS):
            neg_both.append(keep.tile([P, R, D], F32, name=f"neg_both{b}"))
            nc.vector.tensor_tensor(
                neg_both[b][:].rearrange("p r d -> p (r d)"), neg_top[b][:].indirect(lb_t[:]), neg_short[:, b, :], ALU.add
            )

        for c in range(CHUNKS):
            summed = psum.tile([P, P], F32, name="summed", tag=banks[c])
            for d in range(D):
                transpose_add(summed[:], ex[c][:, d, :], d == 0, d == D - 1)
            nc.scalar.copy(mass[c // PER_BLOCK][:, groups(c)], summed[:])

        neg_peak = keep.tile([P, BLOCKS, R], F32, name="neg_peak")
        total = keep.tile([P, BLOCKS, R], F32, name="total")
        ey = []
        for b in range(BLOCKS):
            nc.vector.tensor_reduce(neg_peak[:, b, :], neg_both[b][:], AX.X, ALU.min)
            gap = keep.tile([P, R, D], F32, name=f"gap{b}")
            nc.vector.tensor_tensor(
                gap[:], neg_both[b][:], neg_peak[:, b, :].unsqueeze(2).to_broadcast([P, R, D]), ALU.subtract
            )
            ey.append(keep.tile([P, W], F32, name=f"ey{b}"))
            nc.scalar.activation(ey[b][:], gap[:].rearrange("p r d -> p (r d)"), ACT.Exp, scale=-1.0)
        for b in range(BLOCKS):
            term = keep.tile([P, R, D], F32, name=f"term{b}")
            nc.vector.tensor_tensor(
                term[:].rearrange("p r d -> p (r d)"), mass[b][:].indirect(lb_t[:]), ey[b][:], ALU.mult
            )
            nc.vector.tensor_reduce(total[:, b, :], term[:], AX.X, ALU.add)

        logs = keep.tile([P, BLOCKS, R], F32, name="logs")
        nc.scalar.activation(logs[:], total[:], ACT.Ln)
        result = keep.tile([P, BLOCKS, R], F32, name="result")
        nc.vector.tensor_tensor(result[:], logs[:], neg_peak[:], ALU.subtract)
        nc.sync.dma_start(out.rearrange("(b p) r -> p b r", p=P), result[:])
